import numpy as np
import ml_dtypes


def mxq(x, axis, fmt="e4m3"):
    dtype, down = {"e4m3": (ml_dtypes.float8_e4m3fn, 7), "e5m2": (ml_dtypes.float8_e5m2, 14)}[fmt]
    v = np.moveaxis(np.asarray(x, np.float32).astype(ml_dtypes.bfloat16).astype(np.float64), axis, -1)
    blocks = v.reshape(v.shape[:-1] + (-1, 32))
    amax = np.abs(blocks).max(-1, keepdims=True)
    byte = np.maximum(np.where(amax > 0, np.frexp(amax)[1] - 1 + 127, 0) - down, 1)
    scale = np.exp2(byte - 127.0)
    codes = (blocks / scale).astype(np.float32).astype(dtype).astype(np.float64)
    return np.moveaxis((codes * scale).reshape(v.shape), -1, axis)


WIDE = False


def mx_kscale(k):
    if not WIDE:
        return np.ones(k)
    levels = np.array([10, -10, 5, -5, 0])
    if k % 512:
        return np.exp2(np.random.permutation(np.resize(levels, k // 32))).repeat(32)
    a = np.empty((k // 512, 16))
    for p in range(k // 512):
        a[p, :8] = np.random.permutation(np.resize(levels, 8))
        for g in range(8):
            far = levels[np.abs(levels - a[p, g]) >= 10]
            a[p, g + 8] = far[np.random.randint(len(far))]
    return np.exp2(a.ravel()).repeat(32)


BF16 = ml_dtypes.bfloat16


def bf(x):
    return np.asarray(x, np.float32).astype(BF16)


def f64(x):
    return np.asarray(x).astype(np.float64)


N, D, E, G = 1024, 1024, 1024, 3


def gained_product(left, right, p_row, q_row):
    return mxq(left * p_row[None, :], 1, "e4m3") @ mxq(q_row[:, None] * right, 0, "e4m3")


def mod_relu(z, b):
    return np.sign(z) * np.maximum(np.abs(z) + b[None, :], 0.0)


def draw0():
    cx = mx_kscale(E)
    c = np.stack([mx_kscale(D) for _ in range(G)])
    h = np.random.standard_normal((N, D))
    x = np.random.standard_normal((N, E)) * cx[None, :]
    a = np.random.standard_normal((D, D)) / np.sqrt(D)
    t = np.random.standard_normal((E, D)) / np.sqrt(E) / cx[:, None]
    p = (1.0 + 0.2 * np.random.standard_normal((G, D))) * c
    q = (1.0 + 0.2 * np.random.standard_normal((G, D))) / c
    b = np.random.uniform(-0.5, -0.1, D)
    return {"h": bf(h), "x": bf(x), "a": bf(a), "t": bf(t), "p": bf(p), "q": bf(q), "b": bf(b)}


def core(h, x, a, t, p, q, b):
    h, x, a, t, p, q, b = f64(h), f64(x), f64(a), f64(t), f64(p), f64(q), f64(b)
    s = a - a.T
    k1 = gained_product(h, s, p[0], q[0])
    s2 = gained_product(s, s, p[1], q[1])
    r = s / 2.0 + s2 / 6.0
    k23 = gained_product(k1, r, p[2], q[2])
    u = mxq(x, 1, "e4m3") @ mxq(t, 0, "e4m3")
    z = h + k1 + k23 + u
    return mod_relu(z, b)


def e4m3fn_bytes(y):
    return np.clip(np.asarray(y, np.float64), -448.0, 448.0).astype(np.float32).astype(ml_dtypes.float8_e4m3fn).view(np.uint8)


def e4m3fn_values(b):
    return np.asarray(b, np.uint8).view(ml_dtypes.float8_e4m3fn).astype(np.float64)


def setup_inputs():
    d = draw0()
    x0 = np.asarray(d['x']).astype(np.float64)
    s = (np.max(np.abs(x0), axis=(0,), keepdims=True) / 448.0).astype(np.float32)
    out = {}
    for k, v in d.items():
        if k == 'x':
            out['x_bytes'] = e4m3fn_bytes(x0 / s.astype(np.float64))
            out['x_scale'] = s
        else:
            out[k] = v
    return out


def reference(h, x_bytes, x_scale, a, t, p, q, b):
    return core(h, e4m3fn_values(x_bytes) * x_scale.astype(np.float64), a, t, p, q, b)

@@ -1,0 +1,324 @@
+from contextlib import ExitStack
+
+import concourse.mybir as mybir
+from concourse.masks import make_identity
+
+F32 = mybir.dt.float32
+BF16 = mybir.dt.bfloat16
+U32 = mybir.dt.uint32
+U8 = mybir.dt.uint8
+FP8 = mybir.dt.float8_e4m3fn
+FP8X4 = mybir.dt.float8_e4m3fn_x4
+ADD = mybir.AluOpType.add
+SUB = mybir.AluOpType.subtract
+MUL = mybir.AluOpType.mult
+MAX = mybir.AluOpType.max
+ACTF = mybir.ActivationFunctionType
+
+P = 128
+D = 1024
+FLOPS = 4 * 2 * 1024 * 1024 * 1024
+
+HOW = {
+    "a2": {(0, 0): "TT", (0, 1): "TT", (1, 0): "TT", (1, 1): "TT"},
+    "b2": {(0, 0): "TT", (0, 1): "DA", (1, 0): "TT", (1, 1): "DA"},
+    "b1": {(0, 0): "AA", (0, 1): "AA", (1, 0): "AA", (1, 1): "AA"},
+}
+X_ON_GPSIMD = (True, True, True, True)
+T_INT = "G"
+
+
+def tile_skewexptaylorrecurrentstep_kernel(tc, h, x_bytes, x_scale, a, t, p, q, b, out):
+    nc = tc.nc
+    with ExitStack() as ctx:
+        keep = ctx.enter_context(tc.tile_pool(name="keep", bufs=1))
+        raw = ctx.enter_context(tc.tile_pool(name="raw", bufs=2))
+        stage = ctx.enter_context(tc.tile_pool(name="stage", bufs=4))
+        work = ctx.enter_context(tc.tile_pool(name="work", bufs=2))
+        psum = ctx.enter_context(tc.psum_pool(name="psum", bufs=2))
+
+        ident = keep.tile([P, P], F32, name="ident")
+        make_identity(nc, ident[:])
+        ident_bf = keep.tile([P, P], BF16, name="ident_bf")
+        nc.vector.tensor_copy(out=ident_bf[:], in_=ident[:])
+        ident_neg = keep.tile([P, P], BF16, name="ident_neg")
+        nc.vector.tensor_scalar(out=ident_neg[:], in0=ident[:], scalar1=-1.0, scalar2=None, op0=MUL)
+
+        a_raw = []
+        for g in range(2):
+            ar = raw.tile([P, 4, D], BF16, name="rows", tag="rows", bufs=2)
+            src = a.rearrange("(g p t) n -> g p t n", g=2, t=4)[g]
+            for u in range(2):
+                nc.sync.dma_start(out=ar[:, 2 * u : 2 * u + 2, :], in_=src[:, 2 * u : 2 * u + 2, :])
+            a_raw.append(ar)
+        gp_bf = keep.tile([P, 6, 4], BF16, name="gp_bf")
+        gq_bf = keep.tile([P, 6, 4], BF16, name="gq_bf")
+        nc.sync.dma_start(out=gp_bf[:], in_=p.rearrange("i (g p t) -> p (i g) t", g=2, t=4))
+        nc.sync.dma_start(out=gq_bf[:], in_=q.rearrange("i (g p t) -> p (i g) t", g=2, t=4))
+        h_sb = keep.tile([P, 8, D], BF16, name="h_sb")
+        h_view = h.rearrange("(p c) k -> p c k", c=8)
+        for i in range(4):
+            nc.sync.dma_start(out=h_sb[:, 2 * i : 2 * i + 2, :], in_=h_view[:, 2 * i : 2 * i + 2, :])
+        xs_bc = keep.tile([P, D], F32, name="xs_bc")
+        nc.sync.dma_start(out=xs_bc[:], in_=x_scale.rearrange("o k -> (o k)").partition_broadcast(P))
+        x_view = x_bytes.rearrange("(p c) k -> p c k", c=8)
+        x_u8 = []
+        for i in range(4):
+            xb = keep.tile([P, 2, D], U8, name="x_u8_%d" % i)
+            nc.sync.dma_start(out=xb[:], in_=x_view[:, 2 * i : 2 * i + 2, :])
+            x_u8.append(xb)
+        b_bc = keep.tile([P, D], BF16, name="b_bc")
+        nc.sync.dma_start(out=b_bc[:], in_=b.partition_broadcast(P))
+
+        gp_f = keep.tile([P, 6, 4], F32, name="gp_f")
+        gq_f = keep.tile([P, 6, 4], F32, name="gq_f")
+        nc.vector.tensor_copy(out=gp_f[:], in_=gp_bf[:])
+        nc.vector.tensor_copy(out=gq_f[:], in_=gq_bf[:])
+        q2_half = keep.tile([P, 2, 4], F32, name="q2_half")
+        nc.vector.tensor_scalar(out=q2_half[:], in0=gq_f[:, 4:6, :], scalar1=0.5, scalar2=None, op0=MUL)
+        q2_sixth = keep.tile([P, 2, 4], F32, name="q2_sixth")
+        nc.vector.tensor_scalar(out=q2_sixth[:], in0=gq_f[:, 4:6, :], scalar1=-1.0 / 6.0, scalar2=None, op0=MUL)
+
+        def codes(name, width=D):
+            w = keep.tile([P, 2, width], U32, name=name + "_w", align_bytes=64)
+            s = keep.tile([P, 2, width], U8, name=name + "_s", align_bytes=64)
+            return w, s
+
+        a1 = codes("a1")
+        a2 = codes("a2")
+        a3 = codes("a3")
+        xq = codes("xq")
+        b1 = codes("b1")
+        tq = codes("tq")
+        b2 = [codes("b2_0", 512), codes("b2_1", 512)]
+        b3 = [codes("b3_0", 512), codes("b3_1", 512)]
+
+        def quantize(dst, g, lo, width, src):
+            nc.vector.quantize_mx(
+                out=dst[0][:, g, lo : lo + width].bitcast(FP8X4),
+                scales=dst[1][:, g, lo : lo + width],
+                in_=src,
+            )
+
+        def mm(out_ap, lhs, l0, rhs, r0, n, start=True, stop=True):
+            for g in range(2):
+                nc.tensor.matmul_mx(
+                    out=out_ap,
+                    lhsT=lhs[0][:, g, l0 : l0 + P].bitcast(FP8X4),
+                    lhsT_scale=lhs[1][:, g, l0 : l0 + P],
+                    rhs=rhs[0][:, g, r0 : r0 + n].bitcast(FP8X4),
+                    rhs_scale=rhs[1][:, g, r0 : r0 + n],
+                    start=start and g == 0,
+                    stop=stop and g == 1,
+                )
+
+        def interleave(eng, st, pl):
+            dst = st[:].rearrange("p (c i t) -> p c t i", i=4, t=4)
+            src = pl[:].rearrange("p t (c i) -> p c t i", i=4)
+            if eng == "A":
+                nc.scalar.copy(out=dst, in_=src)
+            elif eng == "D":
+                nc.vector.tensor_copy(out=dst, in_=src)
+            else:
+                nc.gpsimd.tensor_scalar(out=dst, in0=src, scalar1=1.0, scalar2=0.0, op0=MUL, op1=ADD)
+
+        s = keep.tile([P, 2, 4, D], F32, name="s")
+        for g, gc in ((0, 0), (0, 1), (1, 0), (1, 1)):
+            for tt in range(4):
+                bank = psum.tile([P, 512], F32, name="tr", tag="tr", bufs=3)
+                for tc2 in range(4):
+                    nc.tensor.matmul(
+                        bank[:, P * tc2 : P * tc2 + P],
+                        lhsT=ident_bf[:],
+                        rhs=a_raw[g][:, tt, 512 * gc + tc2 : 512 * gc + 512 : 4],
+                        start=True,
+                        stop=False,
+                    )
+                    nc.tensor.matmul(
+                        bank[:, P * tc2 : P * tc2 + P],
+                        lhsT=a_raw[gc][:, tc2, 512 * g + tt : 512 * g + 512 : 4],
+                        rhs=ident_neg[:],
+                        start=False,
+                        stop=True,
+                    )
+                nc.scalar.copy(out=s[:, g, tt, 512 * gc : 512 * gc + 512], in_=bank[:])
+
+        def gain_ap(gain, row, n):
+            return gain[:, row, :].rearrange("p (u e) -> p u e", u=2).unsqueeze(1).to_broadcast([P, n, 2, 2])
+
+        def gained_s(name, dst, lo, g, gc, gain_bf, gain_f, row):
+            how = HOW[name][(g, gc)]
+            st = stage.tile([P, 2048], BF16, name="st", tag="st", bufs=3, align_bytes=64)
+            s_blk = s[:, g, :, 512 * gc : 512 * gc + 512]
+            if how == "TT":
+                nc.vector.tensor_tensor(
+                    out=st[:].rearrange("p (n t) -> p n t", t=4),
+                    in0=s_blk.rearrange("p t n -> p n t"),
+                    in1=gain_bf[:, row, :].unsqueeze(1).to_broadcast([P, 512, 4]),
+                    op=MUL,
+                )
+            else:
+                pl = stage.tile([P, 4, 512], BF16, name="pl", tag="pl", bufs=2, align_bytes=64)
+                for tt in range(4):
+                    col = gain_f[:, row, tt : tt + 1]
+                    if how[0] == "A":
+                        nc.scalar.activation(out=pl[:, tt, :], in_=s_blk[:, tt, :], func=ACTF.Copy, scale=col)
+                    elif how[0] == "D":
+                        nc.vector.tensor_scalar(out=pl[:, tt, :], in0=s_blk[:, tt, :], scalar1=col, scalar2=None, op0=MUL)
+                    else:
+                        nc.gpsimd.tensor_scalar(
+                            out=pl[:, tt, :], in0=s_blk[:, tt, :], scalar1=col, scalar2=0.0, op0=MUL, op1=ADD
+                        )
+                interleave(how[1], st, pl)
+            quantize(dst, g, lo, 512, st[:])
+
+        for g, gc in ((0, 0), (0, 1), (1, 0), (1, 1)):
+            gained_s("a2", a2, 512 * gc, g, gc, gp_bf, gp_f, 2 + g)
+            gained_s("b2", b2[gc], 0, g, gc, gq_bf, gq_f, 2 + g)
+        for g, gc in ((0, 0), (1, 0), (0, 1), (1, 1)):
+            gained_s("b1", b1, 512 * gc, g, gc, gq_bf, gq_f, g)
+
+        def transposed_pair(rows, g):
+            bank = psum.tile([P, 512], F32, name="tr", tag="tr", bufs=3)
+            for j in range(2):
+                words = rows[j].bitcast(F32)
+                for u in range(2):
+                    nc.tensor.transpose(
+                        bank[:, 256 * u + P * j : 256 * u + P * j + P],
+                        words[:, 256 * g + u : 256 * (g + 1) : 2],
+                        ident[:],
+                    )
+            return bank
+
+        def x_pair(i):
+            xw = []
+            for j in range(2):
+                sc = work.tile([P, D], BF16, name="xsc", tag="xsc", bufs=3)
+                if X_ON_GPSIMD[i]:
+                    wide = work.tile([P, D], BF16, name="xwide", tag="xwide", bufs=2)
+                    nc.scalar.copy(out=wide[:], in_=x_u8[i][:, j, :].bitcast(FP8))
+                    nc.gpsimd.tensor_tensor(out=sc[:], in0=wide[:], in1=xs_bc[:], op=MUL)
+                else:
+                    nc.vector.tensor_tensor(out=sc[:], in0=x_u8[i][:, j, :].bitcast(FP8), in1=xs_bc[:], op=MUL)
+                xw.append(sc[:])
+            for g in range(2):
+                bank = transposed_pair(xw, g)
+                st = stage.tile([P, 1024], BF16, name="st1", tag="st1", bufs=3, align_bytes=64)
+                nc.scalar.copy(
+                    out=st[:].bitcast(F32).rearrange("p (n u) -> p n u", u=2),
+                    in_=bank[:].rearrange("p (u n) -> p n u", u=2),
+                )
+                quantize(xq, g, 256 * i, 256, st[:])
+
+        def h_pair(i):
+            for g in range(2):
+                bank = transposed_pair([h_sb[:, 2 * i, :], h_sb[:, 2 * i + 1, :]], g)
+                st = stage.tile([P, 1024], BF16, name="st1", tag="st1", bufs=3, align_bytes=64)
+                nc.vector.tensor_tensor(
+                    out=st[:].rearrange("p (n u e) -> p n u e", u=2, e=2),
+                    in0=bank[:].bitcast(BF16).rearrange("p (u n e) -> p n u e", u=2, e=2),
+                    in1=gain_ap(gp_bf, g, 256),
+                    op=MUL,
+                )
+                quantize(a1, g, 256 * i, 256, st[:])
+
+        for i in range(4):
+            h_pair(i)
+
+        def r_block(g, gc):
+            pl = stage.tile([P, 4, 512], BF16, name="pl3", tag="pl", bufs=2, align_bytes=64)
+            qs = work.tile([P, 4, 512], F32, name="qs", tag="qs", bufs=1)
+            for tt in range(4):
+                nc.gpsimd.tensor_scalar(
+                    out=qs[:, tt, :],
+                    in0=s[:, g, tt, 512 * gc : 512 * gc + 512],
+                    scalar1=q2_half[:, g, tt : tt + 1],
+                    scalar2=0.0,
+                    op0=MUL,
+                    op1=ADD,
+                )
+                bank = psum.tile([P, 512], F32, name="mm", tag="mm", bufs=5)
+                mm(bank[:], a2, 512 * g + P * tt, b2[gc], 0, 512)
+                nc.vector.scalar_tensor_tensor(
+                    out=pl[:, tt, :], in0=bank[:], scalar=q2_sixth[:, g, tt : tt + 1], in1=qs[:, tt, :], op0=MUL, op1=ADD
+                )
+            st = stage.tile([P, 2048], BF16, name="st", tag="st", bufs=3, align_bytes=64)
+            interleave("A", st, pl)
+            quantize(b3[gc], g, 0, 512, st[:])
+
+        def k1_four(g, c4):
+            st = stage.tile([P, 2048], BF16, name="st", tag="st", bufs=3, align_bytes=64)
+            for j in range(4):
+                c = 4 * c4 + j
+                bank = psum.tile([P, 512], F32, name="mm", tag="mm", bufs=5)
+                for tt in range(4):
+                    mm(bank[:, P * tt : P * tt + P], b1, 512 * g + P * tt, a1, P * c, P)
+                nc.vector.tensor_tensor(
+                    out=st[:, 512 * j : 512 * j + 512].rearrange("p (n t) -> p n t", t=4),
+                    in0=bank[:].rearrange("p (t n) -> p n t", t=4),
+                    in1=gp_bf[:, 4 + g, :].unsqueeze(1).to_broadcast([P, P, 4]),
+                    op=MUL,
+                )
+            quantize(a3, g, 512 * c4, 512, st[:])
+
+        t_raw = []
+        t_view = t.rearrange("(g p t) n -> g p t n", g=2, t=4)
+        for g in range(2):
+            tr = raw.tile([P, 4, D], BF16, name="rows", tag="rows", bufs=2)
+            nc.sync.dma_start(out=tr[:], in_=t_view[g])
+            t_raw.append(tr)
+
+        def t_block(g, gc):
+            st = stage.tile([P, 2048], BF16, name="st", tag="st", bufs=3, align_bytes=64)
+            dst = st[:].rearrange("p (c m t) -> p c m t", c=4, t=4)
+            src = t_raw[g][:, :, 512 * gc : 512 * gc + 512].rearrange("p t (m c) -> p c m t", c=4)
+            if T_INT == "A":
+                nc.scalar.copy(out=dst, in_=src)
+            else:
+                nc.gpsimd.tensor_scalar(out=dst, in0=src, scalar1=1.0, scalar2=0.0, op0=MUL, op1=ADD)
+            quantize(tq, g, 512 * gc, 512, st[:])
+
+        r_block(0, 0)
+        r_block(1, 0)
+        x_pair(0)
+        k1_four(0, 0)
+        k1_four(1, 0)
+        x_pair(1)
+        t_block(0, 0)
+        t_block(1, 0)
+        k1_four(0, 1)
+        x_pair(2)
+        k1_four(1, 1)
+        x_pair(3)
+        r_block(0, 1)
+        r_block(1, 1)
+        t_block(0, 1)
+        t_block(1, 1)
+
+        out_view = out.rearrange("(p c) j -> p c j", c=8)
+        for jh in range(2):
+            cols = slice(512 * jh, 512 * jh + 512)
+            for c2 in range(4):
+                z = work.tile([P, 2, 512], F32, name="z", tag="z", bufs=2)
+                for j in range(2):
+                    c = 2 * c2 + j
+                    bank = psum.tile([P, 512], F32, name="mm", tag="mm", bufs=5)
+                    mm(bank[:], xq, P * c, tq, 512 * jh, 512, stop=False)
+                    mm(bank[:], a1, P * c, b1, 512 * jh, 512, start=False, stop=False)
+                    mm(bank[:], a3, P * c, b3[jh], 0, 512, start=False)
+                    nc.vector.tensor_tensor(
+                        out=z[:, j, :].rearrange("p (m t) -> p m t", t=4),
+                        in0=bank[:].rearrange("p (t m) -> p m t", t=4),
+                        in1=h_sb[:, c, cols].rearrange("p (m t) -> p m t", t=4),
+                        op=ADD,
+                    )
+                ab = work.tile([P, 2, 512], F32, name="ab", tag="ab", bufs=2)
+                nc.scalar.activation(out=ab[:], in_=z[:], func=ACTF.Abs)
+                sg = work.tile([P, 2, 512], BF16, name="sg", tag="sg", bufs=2)
+                nc.scalar.activation(out=sg[:], in_=z[:], func=ACTF.Sign)
+                nc.vector.tensor_tensor(
+                    out=ab[:], in0=ab[:], in1=b_bc[:, cols].unsqueeze(1).to_broadcast([P, 2, 512]), op=ADD
+                )
+                ov = work.tile([P, 2, 512], F32, name="ov", tag="ov", bufs=2)
+                nc.vector.scalar_tensor_tensor(out=ov[:], in0=ab[:], scalar=0.0, in1=sg[:], op0=MAX, op1=MUL)
+                nc.sync.dma_start(out=out_view[:, 2 * c2 : 2 * c2 + 2, cols], in_=ov[:])

@@ -10,7 +10,6 @@ U8 = mybir.dt.uint8
 FP8 = mybir.dt.float8_e4m3fn
 FP8X4 = mybir.dt.float8_e4m3fn_x4
 ADD = mybir.AluOpType.add
-SUB = mybir.AluOpType.subtract
 MUL = mybir.AluOpType.mult
 MAX = mybir.AluOpType.max
 ACTF = mybir.ActivationFunctionType
@@ -19,23 +18,26 @@ P = 128
 D = 1024
 FLOPS = 4 * 2 * 1024 * 1024 * 1024
 
-HOW = {
-    "a2": {(0, 0): "TT", (0, 1): "TT", (1, 0): "TT", (1, 1): "TT"},
-    "b2": {(0, 0): "TT", (0, 1): "DA", (1, 0): "TT", (1, 1): "DA"},
-    "b1": {(0, 0): "AA", (0, 1): "AA", (1, 0): "AA", (1, 1): "AA"},
-}
-X_ON_GPSIMD = (True, True, True, True)
-T_INT = "G"
+B2_ON_S = {(1, 1)}
+K1_ON_S = set()
+FIXED = 16
+V_AFTER_V = 230
+AFTER = 75
+T_AFTER = 180
+SWITCH = 120
+LOAD_LATENCY = 2100
+LOAD_RATE = 492000
 
 
 def tile_skewexptaylorrecurrentstep_kernel(tc, h, x_bytes, x_scale, a, t, p, q, b, out):
     nc = tc.nc
     with ExitStack() as ctx:
         keep = ctx.enter_context(tc.tile_pool(name="keep", bufs=1))
-        raw = ctx.enter_context(tc.tile_pool(name="raw", bufs=2))
-        stage = ctx.enter_context(tc.tile_pool(name="stage", bufs=4))
-        work = ctx.enter_context(tc.tile_pool(name="work", bufs=2))
+        pool = ctx.enter_context(tc.tile_pool(name="pool", bufs=2))
         psum = ctx.enter_context(tc.psum_pool(name="psum", bufs=2))
+        ctx.enter_context(tc.manual_schedule())
+
+        BUFS = {"st": 3, "sta": 2, "pl": 2, "st1": 3, "xsc": 4, "qs": 2, "z": 2, "tr": 3, "mm": 5}
 
         ident = keep.tile([P, P], F32, name="ident")
         make_identity(nc, ident[:])
@@ -44,40 +46,52 @@ def tile_skewexptaylorrecurrentstep_kernel(tc, h, x_bytes, x_scale, a, t, p, q, 
         ident_neg = keep.tile([P, P], BF16, name="ident_neg")
         nc.vector.tensor_scalar(out=ident_neg[:], in0=ident[:], scalar1=-1.0, scalar2=None, op0=MUL)
 
-        a_raw = []
-        for g in range(2):
-            ar = raw.tile([P, 4, D], BF16, name="rows", tag="rows", bufs=2)
-            src = a.rearrange("(g p t) n -> g p t n", g=2, t=4)[g]
-            for u in range(2):
-                nc.sync.dma_start(out=ar[:, 2 * u : 2 * u + 2, :], in_=src[:, 2 * u : 2 * u + 2, :])
-            a_raw.append(ar)
         gp_bf = keep.tile([P, 6, 4], BF16, name="gp_bf")
         gq_bf = keep.tile([P, 6, 4], BF16, name="gq_bf")
-        nc.sync.dma_start(out=gp_bf[:], in_=p.rearrange("i (g p t) -> p (i g) t", g=2, t=4))
-        nc.sync.dma_start(out=gq_bf[:], in_=q.rearrange("i (g p t) -> p (i g) t", g=2, t=4))
+        nc.scalar.dma_start(out=gp_bf[:], in_=p.rearrange("i (g p t) -> p (i g) t", g=2, t=4))
+        nc.scalar.dma_start(out=gq_bf[:], in_=q.rearrange("i (g p t) -> p (i g) t", g=2, t=4))
         h_sb = keep.tile([P, 8, D], BF16, name="h_sb")
         h_view = h.rearrange("(p c) k -> p c k", c=8)
-        for i in range(4):
-            nc.sync.dma_start(out=h_sb[:, 2 * i : 2 * i + 2, :], in_=h_view[:, 2 * i : 2 * i + 2, :])
-        xs_bc = keep.tile([P, D], F32, name="xs_bc")
-        nc.sync.dma_start(out=xs_bc[:], in_=x_scale.rearrange("o k -> (o k)").partition_broadcast(P))
         x_view = x_bytes.rearrange("(p c) k -> p c k", c=8)
-        x_u8 = []
-        for i in range(4):
-            xb = keep.tile([P, 2, D], U8, name="x_u8_%d" % i)
-            nc.sync.dma_start(out=xb[:], in_=x_view[:, 2 * i : 2 * i + 2, :])
-            x_u8.append(xb)
+        rows = [keep.tile([P, 4, D], BF16, name="rows_%d" % g) for g in range(2)]
+        x_u8 = [keep.tile([P, 2, D], U8, name="x_u8_%d" % i) for i in range(4)]
+        xs_bc = keep.tile([P, D], F32, name="xs_bc")
         b_bc = keep.tile([P, D], BF16, name="b_bc")
-        nc.sync.dma_start(out=b_bc[:], in_=b.partition_broadcast(P))
+        done = {}
+        moved = [0]
+
+        def load(name, dst, src, nbytes):
+            nc.sync.dma_start(out=dst, in_=src)
+            moved[0] += nbytes
+            done[name] = LOAD_LATENCY + moved[0] // (LOAD_RATE // 1000)
+
+        def load_rows(name, src, g):
+            view = src.rearrange("(g p t) n -> g p t n", g=2, t=4)[g]
+            for u in range(2):
+                load((name, g), rows[g][:, 2 * u : 2 * u + 2, :], view[:, 2 * u : 2 * u + 2, :], 512 * 1024)
+
+        def load_h(i):
+            load(("h_in", i), h_sb[:, 2 * i : 2 * i + 2, :], h_view[:, 2 * i : 2 * i + 2, :], 512 * 1024)
+
+        load_h(0)
+        load_h(1)
+        load_rows("a_in", a, 0)
+        load_h(2)
+        load_h(3)
+        load_rows("a_in", a, 1)
+        for i in range(4):
+            load(("x_in", i), x_u8[i][:], x_view[:, 2 * i : 2 * i + 2, :], 256 * 1024)
+        load("xs_in", xs_bc[:], x_scale.rearrange("o k -> (o k)").partition_broadcast(P), 512 * 1024)
+        load("b_in", b_bc[:], b.partition_broadcast(P), 256 * 1024)
 
         gp_f = keep.tile([P, 6, 4], F32, name="gp_f")
         gq_f = keep.tile([P, 6, 4], F32, name="gq_f")
+        q2_half = keep.tile([P, 2, 4], F32, name="q2_half")
+        q2_sixth = keep.tile([P, 2, 4], F32, name="q2_sixth")
         nc.vector.tensor_copy(out=gp_f[:], in_=gp_bf[:])
         nc.vector.tensor_copy(out=gq_f[:], in_=gq_bf[:])
-        q2_half = keep.tile([P, 2, 4], F32, name="q2_half")
-        nc.vector.tensor_scalar(out=q2_half[:], in0=gq_f[:, 4:6, :], scalar1=0.5, scalar2=None, op0=MUL)
-        q2_sixth = keep.tile([P, 2, 4], F32, name="q2_sixth")
-        nc.vector.tensor_scalar(out=q2_sixth[:], in0=gq_f[:, 4:6, :], scalar1=-1.0 / 6.0, scalar2=None, op0=MUL)
+        nc.vector.tensor_scalar(out=q2_half[:], in0=gq_bf[:, 4:6, :], scalar1=0.5, scalar2=None, op0=MUL)
+        nc.vector.tensor_scalar(out=q2_sixth[:], in0=gq_bf[:, 4:6, :], scalar1=-1.0 / 6.0, scalar2=None, op0=MUL)
 
         def codes(name, width=D):
             w = keep.tile([P, 2, width], U32, name=name + "_w", align_bytes=64)
@@ -92,13 +106,31 @@ def tile_skewexptaylorrecurrentstep_kernel(tc, h, x_bytes, x_scale, a, t, p, q, 
         tq = codes("tq")
         b2 = [codes("b2_0", 512), codes("b2_1", 512)]
         b3 = [codes("b3_0", 512), codes("b3_1", 512)]
+        s = keep.tile([P, 2, 2, D, 2], F32, name="s")
 
-        def quantize(dst, g, lo, width, src):
-            nc.vector.quantize_mx(
-                out=dst[0][:, g, lo : lo + width].bitcast(FP8X4),
-                scales=dst[1][:, g, lo : lo + width],
-                in_=src,
-            )
+        steps = []
+        tiles = {}
+
+        def step(name, engine, work, needs, run, takes=None, frees=(), kind=None):
+            steps.append((name, engine, work, needs, run, takes, frees, kind))
+
+        def bank(key, tag, dtype=F32):
+            tiles[key] = psum.tile([P, 2048 // (4 if dtype == F32 else 2)], dtype, name=tag, tag=tag, bufs=BUFS[tag])
+            return tiles[key]
+
+        def buf(key, tag, shape, dtype):
+            tiles[key] = pool.tile([P] + shape, dtype, name=tag, tag=tag, bufs=BUFS[tag], align_bytes=64)
+            return tiles[key]
+
+        def quantize(name, needs, dst, g, lo, width, key, tag):
+            def run():
+                nc.vector.quantize_mx(
+                    out=dst[0][:, g, lo : lo + width].bitcast(FP8X4),
+                    scales=dst[1][:, g, lo : lo + width],
+                    in_=tiles[key][:],
+                )
+
+            step(name, "V", width * 4 * 0.264, needs, run, frees=(tag,))
 
         def mm(out_ap, lhs, l0, rhs, r0, n, start=True, stop=True):
             for g in range(2):
@@ -112,213 +144,440 @@ def tile_skewexptaylorrecurrentstep_kernel(tc, h, x_bytes, x_scale, a, t, p, q, 
                     stop=stop and g == 1,
                 )
 
-        def interleave(eng, st, pl):
-            dst = st[:].rearrange("p (c i t) -> p c t i", i=4, t=4)
-            src = pl[:].rearrange("p t (c i) -> p c t i", i=4)
-            if eng == "A":
-                nc.scalar.copy(out=dst, in_=src)
-            elif eng == "D":
-                nc.vector.tensor_copy(out=dst, in_=src)
-            else:
-                nc.gpsimd.tensor_scalar(out=dst, in0=src, scalar1=1.0, scalar2=0.0, op0=MUL, op1=ADD)
-
-        s = keep.tile([P, 2, 4, D], F32, name="s")
-        for g, gc in ((0, 0), (0, 1), (1, 0), (1, 1)):
-            for tt in range(4):
-                bank = psum.tile([P, 512], F32, name="tr", tag="tr", bufs=3)
-                for tc2 in range(4):
-                    nc.tensor.matmul(
-                        bank[:, P * tc2 : P * tc2 + P],
-                        lhsT=ident_bf[:],
-                        rhs=a_raw[g][:, tt, 512 * gc + tc2 : 512 * gc + 512 : 4],
-                        start=True,
-                        stop=False,
-                    )
-                    nc.tensor.matmul(
-                        bank[:, P * tc2 : P * tc2 + P],
-                        lhsT=a_raw[gc][:, tc2, 512 * g + tt : 512 * g + 512 : 4],
-                        rhs=ident_neg[:],
-                        start=False,
-                        stop=True,
-                    )
-                nc.scalar.copy(out=s[:, g, tt, 512 * gc : 512 * gc + 512], in_=bank[:])
-
         def gain_ap(gain, row, n):
             return gain[:, row, :].rearrange("p (u e) -> p u e", u=2).unsqueeze(1).to_broadcast([P, n, 2, 2])
 
-        def gained_s(name, dst, lo, g, gc, gain_bf, gain_f, row):
-            how = HOW[name][(g, gc)]
-            st = stage.tile([P, 2048], BF16, name="st", tag="st", bufs=3, align_bytes=64)
-            s_blk = s[:, g, :, 512 * gc : 512 * gc + 512]
-            if how == "TT":
-                nc.vector.tensor_tensor(
-                    out=st[:].rearrange("p (n t) -> p n t", t=4),
-                    in0=s_blk.rearrange("p t n -> p n t"),
-                    in1=gain_bf[:, row, :].unsqueeze(1).to_broadcast([P, 512, 4]),
-                    op=MUL,
-                )
-            else:
-                pl = stage.tile([P, 4, 512], BF16, name="pl", tag="pl", bufs=2, align_bytes=64)
-                for tt in range(4):
-                    col = gain_f[:, row, tt : tt + 1]
-                    if how[0] == "A":
-                        nc.scalar.activation(out=pl[:, tt, :], in_=s_blk[:, tt, :], func=ACTF.Copy, scale=col)
-                    elif how[0] == "D":
-                        nc.vector.tensor_scalar(out=pl[:, tt, :], in0=s_blk[:, tt, :], scalar1=col, scalar2=None, op0=MUL)
-                    else:
-                        nc.gpsimd.tensor_scalar(
-                            out=pl[:, tt, :], in0=s_blk[:, tt, :], scalar1=col, scalar2=0.0, op0=MUL, op1=ADD
-                        )
-                interleave(how[1], st, pl)
-            quantize(dst, g, lo, 512, st[:])
-
-        for g, gc in ((0, 0), (0, 1), (1, 0), (1, 1)):
-            gained_s("a2", a2, 512 * gc, g, gc, gp_bf, gp_f, 2 + g)
-            gained_s("b2", b2[gc], 0, g, gc, gq_bf, gq_f, 2 + g)
-        for g, gc in ((0, 0), (1, 0), (0, 1), (1, 1)):
-            gained_s("b1", b1, 512 * gc, g, gc, gq_bf, gq_f, g)
-
-        def transposed_pair(rows, g):
-            bank = psum.tile([P, 512], F32, name="tr", tag="tr", bufs=3)
+        def transposes(key, words, g):
+            dst = bank(key, "tr")
             for j in range(2):
-                words = rows[j].bitcast(F32)
                 for u in range(2):
                     nc.tensor.transpose(
-                        bank[:, 256 * u + P * j : 256 * u + P * j + P],
-                        words[:, 256 * g + u : 256 * (g + 1) : 2],
+                        dst[:, 256 * u + P * j : 256 * u + P * j + P],
+                        words[j][:, 256 * g + u : 256 * (g + 1) : 2],
                         ident[:],
                     )
-            return bank
 
-        def x_pair(i):
-            xw = []
-            for j in range(2):
-                sc = work.tile([P, D], BF16, name="xsc", tag="xsc", bufs=3)
-                if X_ON_GPSIMD[i]:
-                    wide = work.tile([P, D], BF16, name="xwide", tag="xwide", bufs=2)
-                    nc.scalar.copy(out=wide[:], in_=x_u8[i][:, j, :].bitcast(FP8))
-                    nc.gpsimd.tensor_tensor(out=sc[:], in0=wide[:], in1=xs_bc[:], op=MUL)
-                else:
-                    nc.vector.tensor_tensor(out=sc[:], in0=x_u8[i][:, j, :].bitcast(FP8), in1=xs_bc[:], op=MUL)
-                xw.append(sc[:])
-            for g in range(2):
-                bank = transposed_pair(xw, g)
-                st = stage.tile([P, 1024], BF16, name="st1", tag="st1", bufs=3, align_bytes=64)
-                nc.scalar.copy(
-                    out=st[:].bitcast(F32).rearrange("p (n u) -> p n u", u=2),
-                    in_=bank[:].rearrange("p (u n) -> p n u", u=2),
-                )
-                quantize(xq, g, 256 * i, 256, st[:])
+        def h_steps(i, g):
+            def turn():
+                transposes(("hT", i, g), [h_sb[:, 2 * i + j, :].bitcast(F32) for j in range(2)], g)
 
-        def h_pair(i):
-            for g in range(2):
-                bank = transposed_pair([h_sb[:, 2 * i, :], h_sb[:, 2 * i + 1, :]], g)
-                st = stage.tile([P, 1024], BF16, name="st1", tag="st1", bufs=3, align_bytes=64)
+            def gain():
                 nc.vector.tensor_tensor(
-                    out=st[:].rearrange("p (n u e) -> p n u e", u=2, e=2),
-                    in0=bank[:].bitcast(BF16).rearrange("p (u n e) -> p n u e", u=2, e=2),
+                    out=buf(("h", i, g), "st1", [1024], BF16)[:].rearrange("p (n u e) -> p n u e", u=2, e=2),
+                    in0=tiles["hT", i, g][:].bitcast(BF16).rearrange("p (u n e) -> p n u e", u=2, e=2),
                     in1=gain_ap(gp_bf, g, 256),
                     op=MUL,
                 )
-                quantize(a1, g, 256 * i, 256, st[:])
 
-        for i in range(4):
-            h_pair(i)
+            step(("hT", i, g), "T", 504, [("h_in", i)], turn, takes="tr", kind="turn")
+            step(("h", i, g), "V", 512, [("hT", i, g)], gain, takes="st1", frees=("tr",))
+            quantize(("hq", i, g), [("h", i, g)], a1, g, 256 * i, 256, ("h", i, g), "st1")
 
-        def r_block(g, gc):
-            pl = stage.tile([P, 4, 512], BF16, name="pl3", tag="pl", bufs=2, align_bytes=64)
-            qs = work.tile([P, 4, 512], F32, name="qs", tag="qs", bufs=1)
-            for tt in range(4):
-                nc.gpsimd.tensor_scalar(
-                    out=qs[:, tt, :],
-                    in0=s[:, g, tt, 512 * gc : 512 * gc + 512],
-                    scalar1=q2_half[:, g, tt : tt + 1],
-                    scalar2=0.0,
+        def s_steps(g, gc, u, half):
+            def product():
+                dst = bank(("sT", g, gc, u, half), "tr")
+                for e in range(2):
+                    row = 2 * u + e
+                    for j in range(2):
+                        col = 2 * half + j
+                        part = dst[:, 256 * e + P * j : 256 * e + P * j + P]
+                        nc.tensor.matmul(
+                            part, lhsT=ident_bf[:], rhs=rows[g][:, row, 512 * gc + col : 512 * gc + 512 : 4], start=True, stop=False
+                        )
+                        nc.tensor.matmul(
+                            part, lhsT=rows[gc][:, col, 512 * g + row : 512 * g + 512 : 4], rhs=ident_neg[:], start=False, stop=True
+                        )
+
+            def copy():
+                lo = 512 * gc + 256 * half
+                nc.scalar.copy(
+                    out=s[:, g, u, lo : lo + 256, :], in_=tiles["sT", g, gc, u, half][:].rearrange("p (e n) -> p n e", e=2)
+                )
+
+            step(("sT", g, gc, u, half), "T", 700, [("a_in", g), ("a_in", gc)], product, takes="tr", kind="plain")
+            step(("s", g, gc, u, half), "S", 512, [("sT", g, gc, u, half)], copy, frees=("tr",))
+
+        def s_block(g, gc):
+            return [("s", g, gc, u, half) for u in range(2) for half in range(2)]
+
+        def gain_on_v(name, dst, lo, g, gc, gain, row):
+            def run():
+                nc.vector.tensor_tensor(
+                    out=buf((name, g, gc), "st", [2048], BF16)[:].rearrange("p (n u e) -> p n u e", u=2, e=2),
+                    in0=s[:, g, :, 512 * gc : 512 * gc + 512, :].rearrange("p u n e -> p n u e"),
+                    in1=gain_ap(gain, row, 512),
+                    op=MUL,
+                )
+
+            step((name, g, gc), "V", 2048, s_block(g, gc), run, takes="st")
+            quantize((name + "q", g, gc), [(name, g, gc)], dst, g, lo, 512, (name, g, gc), "st")
+
+        def interleave(name, key, plane_key, needs, dst, g, lo):
+            def run():
+                nc.scalar.copy(
+                    out=buf(key, "sta", [2048], BF16)[:].rearrange("p (c i t) -> p c t i", i=4, t=4),
+                    in_=tiles[plane_key][:].rearrange("p t (c i) -> p c t i", i=4),
+                )
+
+            step(key, "S", 2390, needs, run, takes="sta", frees=("pl",))
+            quantize((name + "q",) + key[1:], [key], dst, g, lo, 512, key, "sta")
+
+        def gain_on_s(name, dst, lo, g, gc, gain, row):
+            def run():
+                pl = buf((name + "p", g, gc), "pl", [4, 512], BF16)
+                for tt in range(4):
+                    nc.scalar.activation(
+                        out=pl[:, tt, :],
+                        in_=s[:, g, tt // 2, 512 * gc : 512 * gc + 512, tt % 2],
+                        func=ACTF.Copy,
+                        scale=gain[:, row, tt : tt + 1],
+                    )
+
+            step((name + "p", g, gc), "S", 2110, s_block(g, gc), run, takes="pl")
+            interleave(name, (name, g, gc), (name + "p", g, gc), [(name + "p", g, gc)], dst, g, lo)
+
+        def r_steps(g, gc):
+            def scaled_s():
+                qs = buf(("qs", g, gc), "qs", [4, 512], F32)
+                for tt in range(4):
+                    nc.scalar.activation(
+                        out=qs[:, tt, :],
+                        in_=s[:, g, tt // 2, 512 * gc : 512 * gc + 512, tt % 2],
+                        func=ACTF.Copy,
+                        scale=q2_half[:, g, tt : tt + 1],
+                    )
+
+            def product(tt):
+                mm(bank(("rT", g, gc, tt), "mm")[:], a2, 512 * g + P * tt, b2[gc], 0, 512)
+
+            def total(tt):
+                if tt == 0:
+                    buf(("r", g, gc), "pl", [4, 512], BF16)
+                nc.vector.scalar_tensor_tensor(
+                    out=tiles["r", g, gc][:, tt, :],
+                    in0=tiles["rT", g, gc, tt][:],
+                    scalar=q2_sixth[:, g, tt : tt + 1],
+                    in1=tiles["qs", g, gc][:, tt, :],
                     op0=MUL,
                     op1=ADD,
                 )
-                bank = psum.tile([P, 512], F32, name="mm", tag="mm", bufs=5)
-                mm(bank[:], a2, 512 * g + P * tt, b2[gc], 0, 512)
-                nc.vector.scalar_tensor_tensor(
-                    out=pl[:, tt, :], in0=bank[:], scalar=q2_sixth[:, g, tt : tt + 1], in1=qs[:, tt, :], op0=MUL, op1=ADD
-                )
-            st = stage.tile([P, 2048], BF16, name="st", tag="st", bufs=3, align_bytes=64)
-            interleave("A", st, pl)
-            quantize(b3[gc], g, 0, 512, st[:])
 
-        def k1_four(g, c4):
-            st = stage.tile([P, 2048], BF16, name="st", tag="st", bufs=3, align_bytes=64)
-            for j in range(4):
-                c = 4 * c4 + j
-                bank = psum.tile([P, 512], F32, name="mm", tag="mm", bufs=5)
+            step(("qs", g, gc), "S", 2110, s_block(g, gc), scaled_s, takes="qs")
+            quantized = [("a2q", k, g) for k in range(2)] + [("b2q", k, gc) for k in range(2)]
+            for tt in range(4):
+                step(("rT", g, gc, tt), "T", 528, quantized, lambda tt=tt: product(tt), takes="mm", kind="mx")
+                step(
+                    ("r", g, gc, tt),
+                    "V",
+                    512,
+                    [("rT", g, gc, tt), ("qs", g, gc)] + ([("after", ("r", g, gc, tt - 1))] if tt else []),
+                    lambda tt=tt: total(tt),
+                    takes="pl" if tt == 0 else None,
+                    frees=("mm", "qs") if tt == 3 else ("mm",),
+                )
+            interleave("b3", ("b3", g, gc), ("r", g, gc), [("r", g, gc, tt) for tt in range(4)], b3[gc], g, 0)
+
+        def k1_steps(g, c4):
+            left = [("b1q", k, g) for k in range(2)]
+
+            def product(c):
+                dst = bank(("kT", g, c), "mm")
                 for tt in range(4):
-                    mm(bank[:, P * tt : P * tt + P], b1, 512 * g + P * tt, a1, P * c, P)
+                    mm(dst[:, P * tt : P * tt + P], b1, 512 * g + P * tt, a1, P * c, P)
+
+            def gain(c, j):
+                if j == 0:
+                    buf(("k", g, c4), "st", [2048], BF16)
                 nc.vector.tensor_tensor(
-                    out=st[:, 512 * j : 512 * j + 512].rearrange("p (n t) -> p n t", t=4),
-                    in0=bank[:].rearrange("p (t n) -> p n t", t=4),
+                    out=tiles["k", g, c4][:, 512 * j : 512 * j + 512].rearrange("p (n t) -> p n t", t=4),
+                    in0=tiles["kT", g, c][:].rearrange("p (t n) -> p n t", t=4),
                     in1=gp_bf[:, 4 + g, :].unsqueeze(1).to_broadcast([P, P, 4]),
                     op=MUL,
                 )
-            quantize(a3, g, 512 * c4, 512, st[:])
 
-        t_raw = []
-        t_view = t.rearrange("(g p t) n -> g p t n", g=2, t=4)
-        for g in range(2):
-            tr = raw.tile([P, 4, D], BF16, name="rows", tag="rows", bufs=2)
-            nc.sync.dma_start(out=tr[:], in_=t_view[g])
-            t_raw.append(tr)
+            for j in range(4):
+                c = 4 * c4 + j
+                right = [("hq", c // 2, k) for k in range(2)]
+                step(("kT", g, c), "T", 600, left + right, lambda c=c: product(c), takes="mm", kind="mx")
+                step(
+                    ("k", g, c),
+                    "V",
+                    512,
+                    [("kT", g, c)] + ([("after", ("k", g, c - 1))] if j else []),
+                    lambda c=c, j=j: gain(c, j),
+                    takes="st" if j == 0 else None,
+                    frees=("mm",),
+                )
+            quantize(("kq", g, c4), [("k", g, 4 * c4 + j) for j in range(4)], a3, g, 512 * c4, 512, ("k", g, c4), "st")
 
-        def t_block(g, gc):
-            st = stage.tile([P, 2048], BF16, name="st", tag="st", bufs=3, align_bytes=64)
-            dst = st[:].rearrange("p (c m t) -> p c m t", c=4, t=4)
-            src = t_raw[g][:, :, 512 * gc : 512 * gc + 512].rearrange("p t (m c) -> p c m t", c=4)
-            if T_INT == "A":
-                nc.scalar.copy(out=dst, in_=src)
-            else:
-                nc.gpsimd.tensor_scalar(out=dst, in0=src, scalar1=1.0, scalar2=0.0, op0=MUL, op1=ADD)
-            quantize(tq, g, 512 * gc, 512, st[:])
+        def k1_on_s(g, c4):
+            needs = [("b1q", k, g) for k in range(2)] + [("hq", 2 * c4 + i, k) for i in range(2) for k in range(2)]
 
-        r_block(0, 0)
-        r_block(1, 0)
-        x_pair(0)
-        k1_four(0, 0)
-        k1_four(1, 0)
-        x_pair(1)
-        t_block(0, 0)
-        t_block(1, 0)
-        k1_four(0, 1)
-        x_pair(2)
-        k1_four(1, 1)
-        x_pair(3)
-        r_block(0, 1)
-        r_block(1, 1)
-        t_block(0, 1)
-        t_block(1, 1)
+            def product(tt):
+                mm(bank(("kT", g, c4, tt), "mm")[:], b1, 512 * g + P * tt, a1, 512 * c4, 512)
+
+            def gain(tt):
+                if tt == 0:
+                    buf(("kp", g, c4), "pl", [4, 512], BF16)
+                nc.scalar.activation(
+                    out=tiles["kp", g, c4][:, tt, :],
+                    in_=tiles["kT", g, c4, tt][:],
+                    func=ACTF.Copy,
+                    scale=gp_f[:, 4 + g, tt : tt + 1],
+                )
+
+            for tt in range(4):
+                step(("kT", g, c4, tt), "T", 528, needs, lambda tt=tt: product(tt), takes="mm", kind="mx")
+                step(
+                    ("kp", g, c4, tt),
+                    "S",
+                    512,
+                    [("kT", g, c4, tt)] + ([("after", ("kp", g, c4, tt - 1))] if tt else []),
+                    lambda tt=tt: gain(tt),
+                    takes="pl" if tt == 0 else None,
+                    frees=("mm",),
+                )
+            interleave("k", ("kj", g, c4), ("kp", g, c4), [("kp", g, c4, tt) for tt in range(4)], a3, g, 512 * c4)
+
+        def x_steps(i):
+            def scaled(c):
+                nc.vector.tensor_tensor(
+                    out=buf(("xw", c), "xsc", [D], BF16)[:], in0=x_u8[i][:, c % 2, :].bitcast(FP8), in1=xs_bc[:], op=MUL
+                )
+
+            def copy(g):
+                nc.scalar.copy(
+                    out=buf(("x", i, g), "st1", [1024], BF16)[:].bitcast(F32).rearrange("p (n u) -> p n u", u=2),
+                    in_=tiles["xT", i, g][:].rearrange("p (u n) -> p n u", u=2),
+                )
+
+            for c in (2 * i, 2 * i + 1):
+                step(("xw", c), "V", 1024, [("x_in", i), "xs_in"], lambda c=c: scaled(c), takes="xsc")
+            for g in range(2):
+                step(
+                    ("xT", i, g),
+                    "T",
+                    504,
+                    [("xw", 2 * i), ("xw", 2 * i + 1)] + ([("after", ("xT", i, 0))] if g else []),
+                    lambda g=g: transposes(("xT", i, g), [tiles["xw", 2 * i + j][:].bitcast(F32) for j in range(2)], g),
+                    takes="tr",
+                    frees=("xsc", "xsc") if g else (),
+                    kind="turn",
+                )
+                step(("x", i, g), "S", 512, [("xT", i, g)], lambda g=g: copy(g), takes="st1", frees=("tr",))
+                quantize(("xq", i, g), [("x", i, g)], xq, g, 256 * i, 256, ("x", i, g), "st1")
+
+        def t_load(g):
+            step(
+                ("t_in", g),
+                "Q",
+                2000,
+                [("s", k, gc, u, half) for k in range(2) for gc in range(2) for u in range(2) for half in range(2)],
+                lambda: load_rows("t_in", t, g),
+            )
+
+        def t_steps(g, gc):
+            def product(half):
+                dst = bank(("tT", g, gc, half), "tr", BF16)
+                for j in range(2):
+                    nc.tensor.matmul(
+                        dst[:, 512 * j : 512 * j + 512].rearrange("p (m t) -> p m t", t=4),
+                        lhsT=ident_bf[:],
+                        rhs=rows[g][:, :, 512 * gc + 2 * half + j : 512 * gc + 512 : 4].rearrange("p t m -> p m t"),
+                        start=True,
+                        stop=True,
+                    )
+
+            def copy(half):
+                if half == 0:
+                    buf(("t", g, gc), "sta", [2048], BF16)
+                nc.scalar.copy(out=tiles["t", g, gc][:, 1024 * half : 1024 * half + 1024], in_=tiles["tT", g, gc, half][:])
+
+            for half in range(2):
+                step(("tT", g, gc, half), "T", 540, [("t_in", g)], lambda half=half: product(half), takes="tr", kind="plain")
+                step(
+                    ("t", g, gc, half),
+                    "S",
+                    512,
+                    [("tT", g, gc, half)] + ([("after", ("t", g, gc, 0))] if half else []),
+                    lambda half=half: copy(half),
+                    takes=None if half else "sta",
+                    frees=("tr",),
+                )
+            quantize(("tq", g, gc), [("t", g, gc, half) for half in range(2)], tq, g, 512 * gc, 512, ("t", g, gc), "sta")
 
         out_view = out.rearrange("(p c) j -> p c j", c=8)
-        for jh in range(2):
+
+        def z_steps(jh, first, count):
             cols = slice(512 * jh, 512 * jh + 512)
-            for c2 in range(4):
-                z = work.tile([P, 2, 512], F32, name="z", tag="z", bufs=2)
-                for j in range(2):
-                    c = 2 * c2 + j
-                    bank = psum.tile([P, 512], F32, name="mm", tag="mm", bufs=5)
-                    mm(bank[:], xq, P * c, tq, 512 * jh, 512, stop=False)
-                    mm(bank[:], a1, P * c, b1, 512 * jh, 512, start=False, stop=False)
-                    mm(bank[:], a3, P * c, b3[jh], 0, 512, start=False)
-                    nc.vector.tensor_tensor(
-                        out=z[:, j, :].rearrange("p (m t) -> p m t", t=4),
-                        in0=bank[:].rearrange("p (t m) -> p m t", t=4),
-                        in1=h_sb[:, c, cols].rearrange("p (m t) -> p m t", t=4),
-                        op=ADD,
-                    )
-                ab = work.tile([P, 2, 512], F32, name="ab", tag="ab", bufs=2)
-                nc.scalar.activation(out=ab[:], in_=z[:], func=ACTF.Abs)
-                sg = work.tile([P, 2, 512], BF16, name="sg", tag="sg", bufs=2)
-                nc.scalar.activation(out=sg[:], in_=z[:], func=ACTF.Sign)
+            key = (jh, first)
+            last = first + count - 1
+
+            def product(c):
+                dst = bank(("zT", jh, c), "mm")[:]
+                mm(dst, xq, P * c, tq, 512 * jh, 512, stop=False)
+                mm(dst, a1, P * c, b1, 512 * jh, 512, start=False, stop=False)
+                mm(dst, a3, P * c, b3[jh], 0, 512, start=False)
+
+            def total(c):
+                if c == first:
+                    buf(("z",) + key, "z", [count, 512], F32)
                 nc.vector.tensor_tensor(
-                    out=ab[:], in0=ab[:], in1=b_bc[:, cols].unsqueeze(1).to_broadcast([P, 2, 512]), op=ADD
+                    out=tiles[("z",) + key][:, c - first, :].rearrange("p (m t) -> p m t", t=4),
+                    in0=tiles["zT", jh, c][:].rearrange("p (t m) -> p m t", t=4),
+                    in1=h_sb[:, c, cols].rearrange("p (m t) -> p m t", t=4),
+                    op=ADD,
                 )
-                ov = work.tile([P, 2, 512], F32, name="ov", tag="ov", bufs=2)
-                nc.vector.scalar_tensor_tensor(out=ov[:], in0=ab[:], scalar=0.0, in1=sg[:], op0=MAX, op1=MUL)
-                nc.sync.dma_start(out=out_view[:, 2 * c2 : 2 * c2 + 2, cols], in_=ov[:])
+
+            def size():
+                nc.scalar.activation(out=buf(("ab",) + key, "pl", [count, 512], F32)[:], in_=tiles[("z",) + key][:], func=ACTF.Abs)
+
+            def sign():
+                nc.scalar.activation(out=buf(("sg",) + key, "st1", [count, 512], BF16)[:], in_=tiles[("z",) + key][:], func=ACTF.Sign)
+
+            def grow():
+                ab = tiles[("ab",) + key]
+                nc.vector.tensor_tensor(
+                    out=ab[:], in0=ab[:], in1=b_bc[:, cols].unsqueeze(1).to_broadcast([P, count, 512]), op=ADD
+                )
+
+            def finish():
+                ov = buf(("ov",) + key, "st", [count, 512], F32)
+                nc.vector.scalar_tensor_tensor(
+                    out=ov[:], in0=tiles[("ab",) + key][:], scalar=0.0, in1=tiles[("sg",) + key][:], op0=MAX, op1=MUL
+                )
+                nc.sync.dma_start(out=out_view[:, first : last + 1, cols], in_=ov[:])
+
+            for c in range(first, last + 1):
+                needs = [("xq", c // 2, g) for g in range(2)] + [("hq", c // 2, g) for g in range(2)]
+                for g in range(2):
+                    needs += [("tq", g, jh), ("b1q", g, jh), ("kq", g, c // 4), ("b3q", g, jh)]
+                step(("zT", jh, c), "T", 1584, needs, lambda c=c: product(c), takes="mm", kind="mx")
+                step(
+                    ("z", jh, c),
+                    "V",
+                    512,
+                    [("zT", jh, c)] + ([("after", ("z", jh, c - 1))] if c > first else []),
+                    lambda c=c: total(c),
+                    takes="z" if c == first else None,
+                    frees=("mm",),
+                )
+            sums = [("z", jh, c) for c in range(first, last + 1)]
+            step(("ab",) + key, "S", 512 * count, sums, size, takes="pl")
+            step(("sg",) + key, "S", 512 * count, sums + [("after", ("ab",) + key)], sign, takes="st1", frees=("z",))
+            step(("w",) + key, "V", 512 * count, [("ab",) + key], grow)
+            step(("o",) + key, "V", 512 * count, [("w",) + key, ("sg",) + key], finish, takes="st", frees=("pl", "st1", "out"))
+
+        h_steps(1, 0)
+        any(s_steps(0, 0, u, half) for u in range(2) for half in range(2))
+        z_steps(0, 2, 2)
+        h_steps(0, 1)
+        r_steps(0, 0)
+        r_steps(1, 0)
+        h_steps(2, 0)
+        z_steps(1, 7, 1)
+        z_steps(1, 0, 2)
+        h_steps(1, 1)
+        h_steps(3, 0)
+        gain_on_v("b2", b2[0], 0, 1, 0, gq_bf, 3)
+        h_steps(2, 1)
+        gain_on_v("a2", a2, 0, 1, 0, gp_bf, 3)
+        z_steps(1, 2, 2)
+        gain_on_s("b1", b1, 0, 0, 0, gq_f, 0)
+        gain_on_v("a2", a2, 512, 1, 1, gp_bf, 3)
+        gain_on_v("b2", b2[0], 0, 0, 0, gq_bf, 2)
+        h_steps(3, 1)
+        any(s_steps(1, 0, u, half) for u in range(2) for half in range(2))
+        gain_on_v("a2", a2, 0, 0, 0, gp_bf, 2)
+        any(s_steps(0, 1, u, half) for u in range(2) for half in range(2))
+        gain_on_s("b1", b1, 0, 1, 0, gq_f, 1)
+        any(s_steps(1, 1, u, half) for u in range(2) for half in range(2))
+        k1_steps(0, 0)
+        gain_on_s("b1", b1, 512, 1, 1, gq_f, 1)
+        gain_on_v("a2", a2, 512, 0, 1, gp_bf, 2)
+        x_steps(1)
+        gain_on_v("b2", b2[1], 0, 0, 1, gq_bf, 2)
+        gain_on_s("b2", b2[1], 0, 1, 1, gq_f, 3)
+        t_steps(1, 0)
+        z_steps(1, 4, 2)
+        gain_on_s("b1", b1, 512, 0, 1, gq_f, 0)
+        z_steps(0, 0, 2)
+        k1_steps(0, 1)
+        k1_steps(1, 0)
+        r_steps(1, 1)
+        t_steps(0, 1)
+        x_steps(3)
+        x_steps(0)
+        t_steps(0, 0)
+        k1_on_s(1, 1)
+        z_steps(1, 6, 1)
+        x_steps(2)
+        r_steps(0, 1)
+        z_steps(0, 6, 2)
+        t_steps(1, 1)
+        t_load(0)
+        t_load(1)
+        h_steps(0, 0)
+        z_steps(0, 4, 2)
+
+        free = {"V": 0, "S": 0, "T": 0, "Q": 0}
+        maker = {}
+        spare = {}
+        for tag in BUFS:
+            spare[tag] = [0] * BUFS[tag]
+        state = {"kind": "turn"}
+
+        def ready(need, engine):
+            soft = need[0] == "after"
+            name = need[1] if soft else need
+            if name not in done:
+                return None
+            if soft:
+                return 0
+            if name not in maker:
+                return done[name]
+            if maker[name] == engine:
+                return done[name] + (V_AFTER_V if engine in ("V", "S") else 0)
+            return done[name] + (T_AFTER if maker[name] == "T" else AFTER)
+
+        left = list(steps)
+        while left:
+            best = None
+            for item in left:
+                name, engine, work, needs, run, takes, frees, kind = item
+                start = free[engine]
+                if takes is not None:
+                    if not spare[takes]:
+                        continue
+                    start = max(start, spare[takes][0])
+                ok = True
+                for need in needs:
+                    when = ready(need, engine)
+                    if when is None:
+                        ok = False
+                        break
+                    start = max(start, when)
+                if ok and (best is None or start < best[0]):
+                    best = (start, item)
+            start, item = best
+            name, engine, work, needs, run, takes, frees, kind = item
+            left.remove(item)
+            if engine == "T":
+                if "turn" in (kind, state["kind"]) and kind != state["kind"]:
+                    work += SWITCH
+                state["kind"] = kind
+            end = start + work + FIXED
+            run()
+            free[engine] = end if engine != "Q" else start
+            if engine != "Q":
+                done[name] = end
+                maker[name] = engine
+            else:
+                done[name] = end + 4000
+            if takes is not None:
+                spare[takes].pop(0)
+            for tag in frees:
+                if tag == "out":
+                    spare["st"].append(end + 3500)
+                else:
+                    spare[tag].append(end + AFTER)

@@ -19,7 +19,7 @@ D = 1024
 FLOPS = 4 * 2 * 1024 * 1024 * 1024
 
 B2_ON_S = {(1, 1)}
-K1_ON_S = set()
+K1_ON_S = {(1, 1)}
 FIXED = 16
 V_AFTER_V = 230
 AFTER = 75
@@ -468,57 +468,57 @@ def tile_skewexptaylorrecurrentstep_kernel(tc, h, x_bytes, x_scale, a, t, p, q, 
             step(("w",) + key, "V", 512 * count, [("ab",) + key], grow)
             step(("o",) + key, "V", 512 * count, [("w",) + key, ("sg",) + key], finish, takes="st", frees=("pl", "st1", "out"))
 
-        h_steps(1, 0)
         any(s_steps(0, 0, u, half) for u in range(2) for half in range(2))
-        z_steps(0, 2, 2)
-        h_steps(0, 1)
-        r_steps(0, 0)
-        r_steps(1, 0)
-        h_steps(2, 0)
-        z_steps(1, 7, 1)
-        z_steps(1, 0, 2)
-        h_steps(1, 1)
+        h_steps(0, 0)
+        h_steps(1, 0)
         h_steps(3, 0)
-        gain_on_v("b2", b2[0], 0, 1, 0, gq_bf, 3)
-        h_steps(2, 1)
-        gain_on_v("a2", a2, 0, 1, 0, gp_bf, 3)
-        z_steps(1, 2, 2)
-        gain_on_s("b1", b1, 0, 0, 0, gq_f, 0)
-        gain_on_v("a2", a2, 512, 1, 1, gp_bf, 3)
-        gain_on_v("b2", b2[0], 0, 0, 0, gq_bf, 2)
         h_steps(3, 1)
+        h_steps(2, 1)
+        t_load(0)
+        h_steps(1, 1)
+        h_steps(2, 0)
         any(s_steps(1, 0, u, half) for u in range(2) for half in range(2))
         gain_on_v("a2", a2, 0, 0, 0, gp_bf, 2)
-        any(s_steps(0, 1, u, half) for u in range(2) for half in range(2))
-        gain_on_s("b1", b1, 0, 1, 0, gq_f, 1)
         any(s_steps(1, 1, u, half) for u in range(2) for half in range(2))
-        k1_steps(0, 0)
-        gain_on_s("b1", b1, 512, 1, 1, gq_f, 1)
+        any(s_steps(0, 1, u, half) for u in range(2) for half in range(2))
+        h_steps(0, 1)
+        r_steps(0, 0)
+        gain_on_v("b2", b2[0], 0, 0, 0, gq_bf, 2)
+        t_load(1)
         gain_on_v("a2", a2, 512, 0, 1, gp_bf, 2)
-        x_steps(1)
-        gain_on_v("b2", b2[1], 0, 0, 1, gq_bf, 2)
-        gain_on_s("b2", b2[1], 0, 1, 1, gq_f, 3)
-        t_steps(1, 0)
-        z_steps(1, 4, 2)
-        gain_on_s("b1", b1, 512, 0, 1, gq_f, 0)
-        z_steps(0, 0, 2)
+        gain_on_v("a2", a2, 0, 1, 0, gp_bf, 3)
+        gain_on_s("b1", b1, 0, 1, 0, gq_f, 1)
+        gain_on_v("a2", a2, 512, 1, 1, gp_bf, 3)
+        gain_on_s("b1", b1, 0, 0, 0, gq_f, 0)
+        k1_steps(0, 0)
+        gain_on_v("b2", b2[0], 0, 1, 0, gq_bf, 3)
+        gain_on_s("b1", b1, 512, 1, 1, gq_f, 1)
         k1_steps(0, 1)
-        k1_steps(1, 0)
-        r_steps(1, 1)
-        t_steps(0, 1)
-        x_steps(3)
         x_steps(0)
         t_steps(0, 0)
-        k1_on_s(1, 1)
-        z_steps(1, 6, 1)
+        gain_on_s("b1", b1, 512, 0, 1, gq_f, 0)
+        x_steps(1)
+        t_steps(1, 0)
+        r_steps(1, 0)
+        k1_steps(1, 0)
+        z_steps(0, 2, 2)
+        gain_on_v("b2", b2[1], 0, 0, 1, gq_bf, 2)
         x_steps(2)
+        k1_on_s(1, 1)
         r_steps(0, 1)
-        z_steps(0, 6, 2)
-        t_steps(1, 1)
-        t_load(0)
-        t_load(1)
-        h_steps(0, 0)
+        x_steps(3)
         z_steps(0, 4, 2)
+        gain_on_s("b2", b2[1], 0, 1, 1, gq_f, 3)
+        z_steps(0, 0, 2)
+        t_steps(1, 1)
+        r_steps(1, 1)
+        z_steps(1, 4, 2)
+        t_steps(0, 1)
+        z_steps(1, 0, 2)
+        z_steps(0, 6, 2)
+        z_steps(1, 2, 2)
+        z_steps(1, 6, 1)
+        z_steps(1, 7, 1)
 
         free = {"V": 0, "S": 0, "T": 0, "Q": 0}
         maker = {}

from contextlib import ExitStack

import concourse.mybir as mybir
from concourse.masks import make_identity

F32 = mybir.dt.float32
BF16 = mybir.dt.bfloat16
U32 = mybir.dt.uint32
U8 = mybir.dt.uint8
FP8 = mybir.dt.float8_e4m3fn
FP8X4 = mybir.dt.float8_e4m3fn_x4
ADD = mybir.AluOpType.add
MUL = mybir.AluOpType.mult
MAX = mybir.AluOpType.max
ACTF = mybir.ActivationFunctionType

P = 128
D = 1024
FLOPS = 4 * 2 * 1024 * 1024 * 1024

B2_ON_S = {(1, 1)}
K1_ON_S = {(1, 1)}
FIXED = 16
V_AFTER_V = 230
AFTER = 75
T_AFTER = 180
SWITCH = 120
LOAD_LATENCY = 2100
LOAD_RATE = 492000


def tile_skewexptaylorrecurrentstep_kernel(tc, h, x_bytes, x_scale, a, t, p, q, b, out):
    nc = tc.nc
    with ExitStack() as ctx:
        keep = ctx.enter_context(tc.tile_pool(name="keep", bufs=1))
        pool = ctx.enter_context(tc.tile_pool(name="pool", bufs=2))
        psum = ctx.enter_context(tc.psum_pool(name="psum", bufs=2))
        ctx.enter_context(tc.manual_schedule())

        BUFS = {"st": 3, "sta": 2, "pl": 2, "st1": 3, "xsc": 4, "qs": 2, "z": 2, "tr": 3, "mm": 5}

        ident = keep.tile([P, P], F32, name="ident")
        make_identity(nc, ident[:])
        ident_bf = keep.tile([P, P], BF16, name="ident_bf")
        nc.vector.tensor_copy(out=ident_bf[:], in_=ident[:])
        ident_neg = keep.tile([P, P], BF16, name="ident_neg")
        nc.vector.tensor_scalar(out=ident_neg[:], in0=ident[:], scalar1=-1.0, scalar2=None, op0=MUL)

        gp_bf = keep.tile([P, 6, 4], BF16, name="gp_bf")
        gq_bf = keep.tile([P, 6, 4], BF16, name="gq_bf")
        nc.scalar.dma_start(out=gp_bf[:], in_=p.rearrange("i (g p t) -> p (i g) t", g=2, t=4))
        nc.scalar.dma_start(out=gq_bf[:], in_=q.rearrange("i (g p t) -> p (i g) t", g=2, t=4))
        h_sb = keep.tile([P, 8, D], BF16, name="h_sb")
        h_view = h.rearrange("(p c) k -> p c k", c=8)
        x_view = x_bytes.rearrange("(p c) k -> p c k", c=8)
        rows = [keep.tile([P, 4, D], BF16, name="rows_%d" % g) for g in range(2)]
        x_u8 = [keep.tile([P, 2, D], U8, name="x_u8_%d" % i) for i in range(4)]
        xs_bc = keep.tile([P, D], F32, name="xs_bc")
        b_bc = keep.tile([P, D], BF16, name="b_bc")
        done = {}
        moved = [0]

        def load(name, dst, src, nbytes):
            nc.sync.dma_start(out=dst, in_=src)
            moved[0] += nbytes
            done[name] = LOAD_LATENCY + moved[0] // (LOAD_RATE // 1000)

        def load_rows(name, src, g):
            view = src.rearrange("(g p t) n -> g p t n", g=2, t=4)[g]
            for u in range(2):
                load((name, g), rows[g][:, 2 * u : 2 * u + 2, :], view[:, 2 * u : 2 * u + 2, :], 512 * 1024)

        def load_h(i):
            load(("h_in", i), h_sb[:, 2 * i : 2 * i + 2, :], h_view[:, 2 * i : 2 * i + 2, :], 512 * 1024)

        load_h(0)
        load_h(1)
        load_rows("a_in", a, 0)
        load_h(2)
        load_h(3)
        load_rows("a_in", a, 1)
        for i in range(4):
            load(("x_in", i), x_u8[i][:], x_view[:, 2 * i : 2 * i + 2, :], 256 * 1024)
        load("xs_in", xs_bc[:], x_scale.rearrange("o k -> (o k)").partition_broadcast(P), 512 * 1024)
        load("b_in", b_bc[:], b.partition_broadcast(P), 256 * 1024)

        gp_f = keep.tile([P, 6, 4], F32, name="gp_f")
        gq_f = keep.tile([P, 6, 4], F32, name="gq_f")
        q2_half = keep.tile([P, 2, 4], F32, name="q2_half")
        q2_sixth = keep.tile([P, 2, 4], F32, name="q2_sixth")
        nc.vector.tensor_copy(out=gp_f[:], in_=gp_bf[:])
        nc.vector.tensor_copy(out=gq_f[:], in_=gq_bf[:])
        nc.vector.tensor_scalar(out=q2_half[:], in0=gq_bf[:, 4:6, :], scalar1=0.5, scalar2=None, op0=MUL)
        nc.vector.tensor_scalar(out=q2_sixth[:], in0=gq_bf[:, 4:6, :], scalar1=-1.0 / 6.0, scalar2=None, op0=MUL)

        def codes(name, width=D):
            w = keep.tile([P, 2, width], U32, name=name + "_w", align_bytes=64)
            s = keep.tile([P, 2, width], U8, name=name + "_s", align_bytes=64)
            return w, s

        a1 = codes("a1")
        a2 = codes("a2")
        a3 = codes("a3")
        xq = codes("xq")
        b1 = codes("b1")
        tq = codes("tq")
        b2 = [codes("b2_0", 512), codes("b2_1", 512)]
        b3 = [codes("b3_0", 512), codes("b3_1", 512)]
        s = keep.tile([P, 2, 2, D, 2], F32, name="s")

        steps = []
        tiles = {}

        def step(name, engine, work, needs, run, takes=None, frees=(), kind=None):
            steps.append((name, engine, work, needs, run, takes, frees, kind))

        def bank(key, tag, dtype=F32):
            tiles[key] = psum.tile([P, 2048 // (4 if dtype == F32 else 2)], dtype, name=tag, tag=tag, bufs=BUFS[tag])
            return tiles[key]

        def buf(key, tag, shape, dtype):
            tiles[key] = pool.tile([P] + shape, dtype, name=tag, tag=tag, bufs=BUFS[tag], align_bytes=64)
            return tiles[key]

        def quantize(name, needs, dst, g, lo, width, key, tag):
            def run():
                nc.vector.quantize_mx(
                    out=dst[0][:, g, lo : lo + width].bitcast(FP8X4),
                    scales=dst[1][:, g, lo : lo + width],
                    in_=tiles[key][:],
                )

            step(name, "V", width * 4 * 0.264, needs, run, frees=(tag,))

        def mm(out_ap, lhs, l0, rhs, r0, n, start=True, stop=True):
            for g in range(2):
                nc.tensor.matmul_mx(
                    out=out_ap,
                    lhsT=lhs[0][:, g, l0 : l0 + P].bitcast(FP8X4),
                    lhsT_scale=lhs[1][:, g, l0 : l0 + P],
                    rhs=rhs[0][:, g, r0 : r0 + n].bitcast(FP8X4),
                    rhs_scale=rhs[1][:, g, r0 : r0 + n],
                    start=start and g == 0,
                    stop=stop and g == 1,
                )

        def gain_ap(gain, row, n):
            return gain[:, row, :].rearrange("p (u e) -> p u e", u=2).unsqueeze(1).to_broadcast([P, n, 2, 2])

        def transposes(key, words, g):
            dst = bank(key, "tr")
            for j in range(2):
                for u in range(2):
                    nc.tensor.transpose(
                        dst[:, 256 * u + P * j : 256 * u + P * j + P],
                        words[j][:, 256 * g + u : 256 * (g + 1) : 2],
                        ident[:],
                    )

        def h_steps(i, g):
            def turn():
                transposes(("hT", i, g), [h_sb[:, 2 * i + j, :].bitcast(F32) for j in range(2)], g)

            def gain():
                nc.vector.tensor_tensor(
                    out=buf(("h", i, g), "st1", [1024], BF16)[:].rearrange("p (n u e) -> p n u e", u=2, e=2),
                    in0=tiles["hT", i, g][:].bitcast(BF16).rearrange("p (u n e) -> p n u e", u=2, e=2),
                    in1=gain_ap(gp_bf, g, 256),
                    op=MUL,
                )

            step(("hT", i, g), "T", 504, [("h_in", i)], turn, takes="tr", kind="turn")
            step(("h", i, g), "V", 512, [("hT", i, g)], gain, takes="st1", frees=("tr",))
            quantize(("hq", i, g), [("h", i, g)], a1, g, 256 * i, 256, ("h", i, g), "st1")

        def s_steps(g, gc, u, half):
            def product():
                dst = bank(("sT", g, gc, u, half), "tr")
                for e in range(2):
                    row = 2 * u + e
                    for j in range(2):
                        col = 2 * half + j
                        part = dst[:, 256 * e + P * j : 256 * e + P * j + P]
                        nc.tensor.matmul(
                            part, lhsT=ident_bf[:], rhs=rows[g][:, row, 512 * gc + col : 512 * gc + 512 : 4], start=True, stop=False
                        )
                        nc.tensor.matmul(
                            part, lhsT=rows[gc][:, col, 512 * g + row : 512 * g + 512 : 4], rhs=ident_neg[:], start=False, stop=True
                        )

            def copy():
                lo = 512 * gc + 256 * half
                nc.scalar.copy(
                    out=s[:, g, u, lo : lo + 256, :], in_=tiles["sT", g, gc, u, half][:].rearrange("p (e n) -> p n e", e=2)
                )

            step(("sT", g, gc, u, half), "T", 700, [("a_in", g), ("a_in", gc)], product, takes="tr", kind="plain")
            step(("s", g, gc, u, half), "S", 512, [("sT", g, gc, u, half)], copy, frees=("tr",))

        def s_block(g, gc):
            return [("s", g, gc, u, half) for u in range(2) for half in range(2)]

        def gain_on_v(name, dst, lo, g, gc, gain, row):
            def run():
                nc.vector.tensor_tensor(
                    out=buf((name, g, gc), "st", [2048], BF16)[:].rearrange("p (n u e) -> p n u e", u=2, e=2),
                    in0=s[:, g, :, 512 * gc : 512 * gc + 512, :].rearrange("p u n e -> p n u e"),
                    in1=gain_ap(gain, row, 512),
                    op=MUL,
                )

            step((name, g, gc), "V", 2048, s_block(g, gc), run, takes="st")
            quantize((name + "q", g, gc), [(name, g, gc)], dst, g, lo, 512, (name, g, gc), "st")

        def interleave(name, key, plane_key, needs, dst, g, lo):
            def run():
                nc.scalar.copy(
                    out=buf(key, "sta", [2048], BF16)[:].rearrange("p (c i t) -> p c t i", i=4, t=4),
                    in_=tiles[plane_key][:].rearrange("p t (c i) -> p c t i", i=4),
                )

            step(key, "S", 2390, needs, run, takes="sta", frees=("pl",))
            quantize((name + "q",) + key[1:], [key], dst, g, lo, 512, key, "sta")

        def gain_on_s(name, dst, lo, g, gc, gain, row):
            def run():
                pl = buf((name + "p", g, gc), "pl", [4, 512], BF16)
                for tt in range(4):
                    nc.scalar.activation(
                        out=pl[:, tt, :],
                        in_=s[:, g, tt // 2, 512 * gc : 512 * gc + 512, tt % 2],
                        func=ACTF.Copy,
                        scale=gain[:, row, tt : tt + 1],
                    )

            step((name + "p", g, gc), "S", 2110, s_block(g, gc), run, takes="pl")
            interleave(name, (name, g, gc), (name + "p", g, gc), [(name + "p", g, gc)], dst, g, lo)

        def r_steps(g, gc):
            def scaled_s():
                qs = buf(("qs", g, gc), "qs", [4, 512], F32)
                for tt in range(4):
                    nc.scalar.activation(
                        out=qs[:, tt, :],
                        in_=s[:, g, tt // 2, 512 * gc : 512 * gc + 512, tt % 2],
                        func=ACTF.Copy,
                        scale=q2_half[:, g, tt : tt + 1],
                    )

            def product(tt):
                mm(bank(("rT", g, gc, tt), "mm")[:], a2, 512 * g + P * tt, b2[gc], 0, 512)

            def total(tt):
                if tt == 0:
                    buf(("r", g, gc), "pl", [4, 512], BF16)
                nc.vector.scalar_tensor_tensor(
                    out=tiles["r", g, gc][:, tt, :],
                    in0=tiles["rT", g, gc, tt][:],
                    scalar=q2_sixth[:, g, tt : tt + 1],
                    in1=tiles["qs", g, gc][:, tt, :],
                    op0=MUL,
                    op1=ADD,
                )

            step(("qs", g, gc), "S", 2110, s_block(g, gc), scaled_s, takes="qs")
            quantized = [("a2q", k, g) for k in range(2)] + [("b2q", k, gc) for k in range(2)]
            for tt in range(4):
                step(("rT", g, gc, tt), "T", 528, quantized, lambda tt=tt: product(tt), takes="mm", kind="mx")
                step(
                    ("r", g, gc, tt),
                    "V",
                    512,
                    [("rT", g, gc, tt), ("qs", g, gc)] + ([("after", ("r", g, gc, tt - 1))] if tt else []),
                    lambda tt=tt: total(tt),
                    takes="pl" if tt == 0 else None,
                    frees=("mm", "qs") if tt == 3 else ("mm",),
                )
            interleave("b3", ("b3", g, gc), ("r", g, gc), [("r", g, gc, tt) for tt in range(4)], b3[gc], g, 0)

        def k1_steps(g, c4):
            left = [("b1q", k, g) for k in range(2)]

            def product(c):
                dst = bank(("kT", g, c), "mm")
                for tt in range(4):
                    mm(dst[:, P * tt : P * tt + P], b1, 512 * g + P * tt, a1, P * c, P)

            def gain(c, j):
                if j == 0:
                    buf(("k", g, c4), "st", [2048], BF16)
                nc.vector.tensor_tensor(
                    out=tiles["k", g, c4][:, 512 * j : 512 * j + 512].rearrange("p (n t) -> p n t", t=4),
                    in0=tiles["kT", g, c][:].rearrange("p (t n) -> p n t", t=4),
                    in1=gp_bf[:, 4 + g, :].unsqueeze(1).to_broadcast([P, P, 4]),
                    op=MUL,
                )

            for j in range(4):
                c = 4 * c4 + j
                right = [("hq", c // 2, k) for k in range(2)]
                step(("kT", g, c), "T", 600, left + right, lambda c=c: product(c), takes="mm", kind="mx")
                step(
                    ("k", g, c),
                    "V",
                    512,
                    [("kT", g, c)] + ([("after", ("k", g, c - 1))] if j else []),
                    lambda c=c, j=j: gain(c, j),
                    takes="st" if j == 0 else None,
                    frees=("mm",),
                )
            quantize(("kq", g, c4), [("k", g, 4 * c4 + j) for j in range(4)], a3, g, 512 * c4, 512, ("k", g, c4), "st")

        def k1_on_s(g, c4):
            needs = [("b1q", k, g) for k in range(2)] + [("hq", 2 * c4 + i, k) for i in range(2) for k in range(2)]

            def product(tt):
                mm(bank(("kT", g, c4, tt), "mm")[:], b1, 512 * g + P * tt, a1, 512 * c4, 512)

            def gain(tt):
                if tt == 0:
                    buf(("kp", g, c4), "pl", [4, 512], BF16)
                nc.scalar.activation(
                    out=tiles["kp", g, c4][:, tt, :],
                    in_=tiles["kT", g, c4, tt][:],
                    func=ACTF.Copy,
                    scale=gp_f[:, 4 + g, tt : tt + 1],
                )

            for tt in range(4):
                step(("kT", g, c4, tt), "T", 528, needs, lambda tt=tt: product(tt), takes="mm", kind="mx")
                step(
                    ("kp", g, c4, tt),
                    "S",
                    512,
                    [("kT", g, c4, tt)] + ([("after", ("kp", g, c4, tt - 1))] if tt else []),
                    lambda tt=tt: gain(tt),
                    takes="pl" if tt == 0 else None,
                    frees=("mm",),
                )
            interleave("k", ("kj", g, c4), ("kp", g, c4), [("kp", g, c4, tt) for tt in range(4)], a3, g, 512 * c4)

        def x_steps(i):
            def scaled(c):
                nc.vector.tensor_tensor(
                    out=buf(("xw", c), "xsc", [D], BF16)[:], in0=x_u8[i][:, c % 2, :].bitcast(FP8), in1=xs_bc[:], op=MUL
                )

            def copy(g):
                nc.scalar.copy(
                    out=buf(("x", i, g), "st1", [1024], BF16)[:].bitcast(F32).rearrange("p (n u) -> p n u", u=2),
                    in_=tiles["xT", i, g][:].rearrange("p (u n) -> p n u", u=2),
                )

            for c in (2 * i, 2 * i + 1):
                step(("xw", c), "V", 1024, [("x_in", i), "xs_in"], lambda c=c: scaled(c), takes="xsc")
            for g in range(2):
                step(
                    ("xT", i, g),
                    "T",
                    504,
                    [("xw", 2 * i), ("xw", 2 * i + 1)] + ([("after", ("xT", i, 0))] if g else []),
                    lambda g=g: transposes(("xT", i, g), [tiles["xw", 2 * i + j][:].bitcast(F32) for j in range(2)], g),
                    takes="tr",
                    frees=("xsc", "xsc") if g else (),
                    kind="turn",
                )
                step(("x", i, g), "S", 512, [("xT", i, g)], lambda g=g: copy(g), takes="st1", frees=("tr",))
                quantize(("xq", i, g), [("x", i, g)], xq, g, 256 * i, 256, ("x", i, g), "st1")

        def t_load(g):
            step(
                ("t_in", g),
                "Q",
                2000,
                [("s", k, gc, u, half) for k in range(2) for gc in range(2) for u in range(2) for half in range(2)],
                lambda: load_rows("t_in", t, g),
            )

        def t_steps(g, gc):
            def product(half):
                dst = bank(("tT", g, gc, half), "tr", BF16)
                for j in range(2):
                    nc.tensor.matmul(
                        dst[:, 512 * j : 512 * j + 512].rearrange("p (m t) -> p m t", t=4),
                        lhsT=ident_bf[:],
                        rhs=rows[g][:, :, 512 * gc + 2 * half + j : 512 * gc + 512 : 4].rearrange("p t m -> p m t"),
                        start=True,
                        stop=True,
                    )

            def copy(half):
                if half == 0:
                    buf(("t", g, gc), "sta", [2048], BF16)
                nc.scalar.copy(out=tiles["t", g, gc][:, 1024 * half : 1024 * half + 1024], in_=tiles["tT", g, gc, half][:])

            for half in range(2):
                step(("tT", g, gc, half), "T", 540, [("t_in", g)], lambda half=half: product(half), takes="tr", kind="plain")
                step(
                    ("t", g, gc, half),
                    "S",
                    512,
                    [("tT", g, gc, half)] + ([("after", ("t", g, gc, 0))] if half else []),
                    lambda half=half: copy(half),
                    takes=None if half else "sta",
                    frees=("tr",),
                )
            quantize(("tq", g, gc), [("t", g, gc, half) for half in range(2)], tq, g, 512 * gc, 512, ("t", g, gc), "sta")

        out_view = out.rearrange("(p c) j -> p c j", c=8)

        def z_steps(jh, first, count):
            cols = slice(512 * jh, 512 * jh + 512)
            key = (jh, first)
            last = first + count - 1

            def product(c):
                dst = bank(("zT", jh, c), "mm")[:]
                mm(dst, xq, P * c, tq, 512 * jh, 512, stop=False)
                mm(dst, a1, P * c, b1, 512 * jh, 512, start=False, stop=False)
                mm(dst, a3, P * c, b3[jh], 0, 512, start=False)

            def total(c):
                if c == first:
                    buf(("z",) + key, "z", [count, 512], F32)
                nc.vector.tensor_tensor(
                    out=tiles[("z",) + key][:, c - first, :].rearrange("p (m t) -> p m t", t=4),
                    in0=tiles["zT", jh, c][:].rearrange("p (t m) -> p m t", t=4),
                    in1=h_sb[:, c, cols].rearrange("p (m t) -> p m t", t=4),
                    op=ADD,
                )

            def size():
                nc.scalar.activation(out=buf(("ab",) + key, "pl", [count, 512], F32)[:], in_=tiles[("z",) + key][:], func=ACTF.Abs)

            def sign():
                nc.scalar.activation(out=buf(("sg",) + key, "st1", [count, 512], BF16)[:], in_=tiles[("z",) + key][:], func=ACTF.Sign)

            def grow():
                ab = tiles[("ab",) + key]
                nc.vector.tensor_tensor(
                    out=ab[:], in0=ab[:], in1=b_bc[:, cols].unsqueeze(1).to_broadcast([P, count, 512]), op=ADD
                )

            def finish():
                ov = buf(("ov",) + key, "st", [count, 512], F32)
                nc.vector.scalar_tensor_tensor(
                    out=ov[:], in0=tiles[("ab",) + key][:], scalar=0.0, in1=tiles[("sg",) + key][:], op0=MAX, op1=MUL
                )
                nc.sync.dma_start(out=out_view[:, first : last + 1, cols], in_=ov[:])

            for c in range(first, last + 1):
                needs = [("xq", c // 2, g) for g in range(2)] + [("hq", c // 2, g) for g in range(2)]
                for g in range(2):
                    needs += [("tq", g, jh), ("b1q", g, jh), ("kq", g, c // 4), ("b3q", g, jh)]
                step(("zT", jh, c), "T", 1584, needs, lambda c=c: product(c), takes="mm", kind="mx")
                step(
                    ("z", jh, c),
                    "V",
                    512,
                    [("zT", jh, c)] + ([("after", ("z", jh, c - 1))] if c > first else []),
                    lambda c=c: total(c),
                    takes="z" if c == first else None,
                    frees=("mm",),
                )
            sums = [("z", jh, c) for c in range(first, last + 1)]
            step(("ab",) + key, "S", 512 * count, sums, size, takes="pl")
            step(("sg",) + key, "S", 512 * count, sums + [("after", ("ab",) + key)], sign, takes="st1", frees=("z",))
            step(("w",) + key, "V", 512 * count, [("ab",) + key], grow)
            step(("o",) + key, "V", 512 * count, [("w",) + key, ("sg",) + key], finish, takes="st", frees=("pl", "st1", "out"))

        any(s_steps(0, 0, u, half) for u in range(2) for half in range(2))
        h_steps(0, 0)
        h_steps(1, 0)
        h_steps(3, 0)
        h_steps(3, 1)
        h_steps(2, 1)
        t_load(0)
        h_steps(1, 1)
        h_steps(2, 0)
        any(s_steps(1, 0, u, half) for u in range(2) for half in range(2))
        gain_on_v("a2", a2, 0, 0, 0, gp_bf, 2)
        any(s_steps(1, 1, u, half) for u in range(2) for half in range(2))
        any(s_steps(0, 1, u, half) for u in range(2) for half in range(2))
        h_steps(0, 1)
        r_steps(0, 0)
        gain_on_v("b2", b2[0], 0, 0, 0, gq_bf, 2)
        t_load(1)
        gain_on_v("a2", a2, 512, 0, 1, gp_bf, 2)
        gain_on_v("a2", a2, 0, 1, 0, gp_bf, 3)
        gain_on_s("b1", b1, 0, 1, 0, gq_f, 1)
        gain_on_v("a2", a2, 512, 1, 1, gp_bf, 3)
        gain_on_s("b1", b1, 0, 0, 0, gq_f, 0)
        k1_steps(0, 0)
        gain_on_v("b2", b2[0], 0, 1, 0, gq_bf, 3)
        gain_on_s("b1", b1, 512, 1, 1, gq_f, 1)
        k1_steps(0, 1)
        x_steps(0)
        t_steps(0, 0)
        gain_on_s("b1", b1, 512, 0, 1, gq_f, 0)
        x_steps(1)
        t_steps(1, 0)
        r_steps(1, 0)
        k1_steps(1, 0)
        z_steps(0, 2, 2)
        gain_on_v("b2", b2[1], 0, 0, 1, gq_bf, 2)
        x_steps(2)
        k1_on_s(1, 1)
        r_steps(0, 1)
        x_steps(3)
        z_steps(0, 4, 2)
        gain_on_s("b2", b2[1], 0, 1, 1, gq_f, 3)
        z_steps(0, 0, 2)
        t_steps(1, 1)
        r_steps(1, 1)
        z_steps(1, 4, 2)
        t_steps(0, 1)
        z_steps(1, 0, 2)
        z_steps(0, 6, 2)
        z_steps(1, 2, 2)
        z_steps(1, 6, 1)
        z_steps(1, 7, 1)

        free = {"V": 0, "S": 0, "T": 0, "Q": 0}
        maker = {}
        spare = {}
        for tag in BUFS:
            spare[tag] = [0] * BUFS[tag]
        state = {"kind": "turn"}

        def ready(need, engine):
            soft = need[0] == "after"
            name = need[1] if soft else need
            if name not in done:
                return None
            if soft:
                return 0
            if name not in maker:
                return done[name]
            if maker[name] == engine:
                return done[name] + (V_AFTER_V if engine in ("V", "S") else 0)
            return done[name] + (T_AFTER if maker[name] == "T" else AFTER)

        left = list(steps)
        while left:
            best = None
            for item in left:
                name, engine, work, needs, run, takes, frees, kind = item
                start = free[engine]
                if takes is not None:
                    if not spare[takes]:
                        continue
                    start = max(start, spare[takes][0])
                ok = True
                for need in needs:
                    when = ready(need, engine)
                    if when is None:
                        ok = False
                        break
                    start = max(start, when)
                if ok and (best is None or start < best[0]):
                    best = (start, item)
            start, item = best
            name, engine, work, needs, run, takes, frees, kind = item
            left.remove(item)
            if engine == "T":
                if "turn" in (kind, state["kind"]) and kind != state["kind"]:
                    work += SWITCH
                state["kind"] = kind
            end = start + work + FIXED
            run()
            free[engine] = end if engine != "Q" else start
            if engine != "Q":
                done[name] = end
                maker[name] = engine
            else:
                done[name] = end + 4000
            if takes is not None:
                spare[takes].pop(0)
            for tag in frees:
                if tag == "out":
                    spare["st"].append(end + 3500)
                else:
                    spare[tag].append(end + AFTER)
